import numpy as np, ml_dtypes
CORES = [66,74,82,90,194,202,210,218]
N = 8
import mx_ref
BF = ml_dtypes.bfloat16
def cols(t, e):
    v = np.concatenate([t.reshape(128, -1, 4), np.zeros((128, 1, 4), BF)], axis=1)
    return np.ascontiguousarray(v[:, e]).reshape(128, -1)
def cut(t, i, w=512):
    return t[:, w * i:w * i + w]
def tile(rs):
    return np.stack(rs, axis=2).reshape(128, -1).astype(BF)
def pick(q, e):
    c = np.concatenate([q[0].reshape(128, -1, 4), np.zeros((128, 1, 4), np.uint8)], axis=1); s = np.concatenate([q[1], np.ones((16, 1), np.uint8)], axis=1)
    return (np.ascontiguousarray(c[:, e].reshape(128, -1)), np.ascontiguousarray(s[:, e]))
def join(*qs):
    return (np.concatenate([q[0] for q in qs], axis=1), np.concatenate([q[1] for q in qs], axis=1))
def put(q, e, v):
    c, s = q[0].reshape(128, -1, 4).copy(), q[1].copy(); c[:, e] = v[0].reshape(128, -1, 4); s[:, e] = v[1]
    return (c.reshape(128, -1), s)
def pk(c, s):
    return (np.ascontiguousarray(c), mx_ref.live(s))
def emit(q):
    return q[0], q[1]
def decode(q):
    o = []
    for b in range(4):
        e = np.zeros((128, 128, 4), np.float32); e[np.arange(128), np.arange(128), b] = 1
        o.append(mx_ref.matmul(mx_ref.quantize(e.reshape(128, 512).astype(BF)), q))
    return np.stack(o, axis=2).reshape(128, -1)
def f(rng, *shape):
    return mx_ref.flush((rng.standard_normal(shape, dtype=np.float32) * np.exp2(rng.integers(-2, 3, shape[:-1] + (1,)))).astype(BF))
def wide(rng, *shape, cols=0):
    v = rng.standard_normal(shape, dtype=np.float32) * np.exp2(rng.integers(-12, 13, shape)).astype(np.float32)
    if cols: v *= np.repeat(np.exp2(rng.integers(-cols, cols + 1, shape[:-2] + (1, shape[-1] // 4))) * (rng.random(shape[:-2] + (1, shape[-1] // 4)) > 0.0625), 4, axis=-1).astype(np.float32)
    return mx_ref.flush(v.astype(BF))
T, A, KM, CAPP, FA = 128, 32, 48, 16, 2
def big(t):
    t = np.array(t)
    t[np.abs(t.astype(np.float32)) < np.float32(2.0 ** -16)] = 0
    return t
def plain(rng):
    x = np.concatenate([f(rng, N, 128, 4 * A), f(rng, N, 128, 4 * (T - A))], axis=2)
    return {"x": big(x), "w": f(rng, N, 128, 2048), "v": f(rng, N, 128, 512)}
def pull(rng, x, at, who, n=8, bare=False):
    x = np.array(x).reshape(N, 128, T, 4)
    x[:, :n * len(at)] = 0
    for i, (q, a) in enumerate(at):
        if bare: x[q, :, a] = 0
        x[q, n * i:n * i + n, a] = (32 * (1 + rng.random((n, 4)))).astype(np.float32).astype(BF)
        r, j = np.nonzero(who == i)
        x[r, n * i:n * i + n, j] = (8 * (1 + rng.random((len(r), n, 4)))).astype(np.float32).astype(BF)
    return x.reshape(N, 128, 4 * T)
def setup_inputs(rng):
    return plain(rng)
def setup_inputs_crowd(rng):
    d, who = plain(rng), np.full((N, T), -1)
    z, q = int(rng.integers(1, N)), rng.permutation(N)[:2]
    for r in range(N):
        e = A + rng.permutation(T - A)[:KM * 5 // 6 + FA]
        who[r, e] = 0
        who[r, e[:FA]] = 1
    who[z, A:] = rng.integers(0, 2, T - A)
    d["x"] = pull(rng, d["x"], [(int(q[i]), int(rng.integers(0, A))) for i in range(2)], who)
    return d
def setup_inputs_full(rng):
    d, who, o = plain(rng), np.full((N, T), -1), rng.permutation(N)
    g = FA * A // CAPP
    e = np.tile(rng.permutation(A), FA).reshape(g, CAPP)
    for i, s in enumerate(np.sort(o[1:g + 1])):
        who[s, A:A + CAPP] = rng.permutation(e[i])
        who[s, A + CAPP:A + CAPP + 4] = e[-1, -1]
    d["x"] = pull(rng, d["x"], [(int(o[0]), a) for a in range(A)], who, 2, True)
    return d
def setup_inputs_ties(rng):
    d = plain(rng)
    x = np.array(d["x"])
    part = np.arange(128) // 8
    m = rng.permutation(N * A) % (N * A // 4)
    k = cols(np.concatenate([x[q][:, :4 * A] for q in range(N)], axis=1), rng.permutation(N * A)[m])
    k = np.abs(k.astype(np.float32)) * np.repeat(np.where(part[:, None] == m % 16, 2.0 ** -8, 1.0), 4, axis=1)
    k = big(k.astype(np.float32).astype(BF))
    for r in range(N):
        g = rng.permutation(np.arange(T - A) // 7)
        u = cols(np.ascontiguousarray(x[r][:, 4 * A:]), g)
        if r == 0:
            on = part[:, None] == (m[0] + 1 + g % 15) % 16
            u = (-np.abs(u.astype(np.float32)) * np.repeat(on, 4, axis=1)).astype(BF)
        if r == 1:
            u = np.abs(u.astype(np.float32)).reshape(128, T - A, 4)
            o = np.append(0, 1 + rng.permutation(T - A - 1)[KM // 2:])
            u[:, o[::2]] = -0.0
            u[:, o[1::2]] = 0.0
            u = u.astype(BF).reshape(128, -1)
        x[r][:, 4 * A:] = u
        x[r][:, :4 * A] = cut(k, r, 4 * A)
    d["x"] = x
    return d
def setup_inputs_own(rng):
    d = plain(rng)
    x = np.array(d["x"])
    x[:, :, 2 * A:4 * A] = -x[:, :, :2 * A]
    x[(np.arange(128) // (128 // N))[None, :] != np.arange(N)[:, None]] = 0
    d["x"] = x
    return d
def setup_inputs_spread(rng):
    return {**plain(rng), "x": big(wide(rng, N, 128, 4 * T, cols=4))}
def check_inputs(d):
    b = []
    for k in ("x", "w", "v"):
        t = np.abs(d[k].astype(np.float32))
        if not (np.isfinite(t).all() and ((t == 0) | (t >= 2.0 ** -30) & (t <= 2.0 ** 30)).all()): b.append("a value of " + k)
    return b
def choose(x):
    k = np.concatenate([x[q][:, :4 * A] for q in range(N)], axis=1)
    k = [mx_ref.quantize(np.ascontiguousarray(cut(k, i))) for i in range(N * A // 128)]
    goal, took, have = np.full((N, T), -1), np.full((N, A, FA), -1), np.zeros((N, A), int)
    for s in range(N):
        u = mx_ref.quantize(np.ascontiguousarray(x[s][:, 4 * A:]))
        z = np.concatenate([mx_ref.matmul(t, u) for t in k]) + np.float32(0.0)
        best = np.argmax(z, axis=0)
        offers = np.sort(np.argsort(-z.max(axis=0), kind="stable")[:KM])
        stand = np.zeros(N, int)
        for j in offers:
            q, a = best[j] // A, best[j] % A
            if stand[q] == CAPP: continue
            stand[q] += 1
            if have[q, a] == FA: continue
            took[q, a, have[q, a]] = s * T + A + j
            have[q, a] += 1
            goal[s, A + j] = q * T + a
    return goal, took
def reference(x, w, v):
    goal, took = choose(x)
    c = [mx_ref.quantize(np.ascontiguousarray(x[r])) for r in range(N)]
    d = np.concatenate([decode(c[r]).reshape(128, T, 4) for r in range(N)], axis=1)
    h = []
    for q in range(N):
        m = d[:, q * T:q * T + A].copy()
        for t in range(FA):
            a = np.flatnonzero(took[q, :, t] >= 0)
            m[:, a] = m[:, a] + d[:, took[q, a, t]]
        new = mx_ref.quantize(np.ascontiguousarray((m * np.float32(0.5)).reshape(128, -1).astype(BF)))
        a = np.flatnonzero(took[q, :, 0] >= 0)
        k = put(c[q], a, pick(new, a))
        rs = [np.maximum(mx_ref.matmul(mx_ref.quantize(np.ascontiguousarray(cut(w[q], i))), k), np.float32(0.0)) * np.float32(0.0625) for i in range(4)]
        h.append(mx_ref.quantize(np.ascontiguousarray(tile(rs))))
    every = join(*h)
    oc, osc = np.zeros((N, 128, 4 * T), np.uint8), np.zeros((N, 16, T), np.uint8)
    mg, y = np.zeros((N, 1, T), np.float32), np.zeros((N, 128, T), np.float32)
    for s in range(N):
        g = pick(every, np.where(goal[s] >= 0, goal[s], s * T + np.arange(T)))
        oc[s], osc[s] = emit(g)
        mg[s, 0] = goal[s]
        y[s] = mx_ref.matmul(mx_ref.quantize(np.ascontiguousarray(v[s])), g)
    return {"oc": oc, "osc": osc, "mg": mg, "y": y}

@@ -1,0 +1,408 @@
+from concourse.bass import DstId, RemoteDMATransfer
+from concourse.mybir import dt, AluOpType as OP, AxisListType, ActivationFunctionType as AF
+
+N, COLS, A, KM, CAPP = 8, 128, 32, 48, 16
+RUN = 20
+NONE = RUN * N
+BIG = 1e29
+
+SCRATCH = {}
+
+
+def _bufs():
+    def sb(n, w, d="float32"):
+        SCRATCH[n] = ("sbuf", [128, w], d)
+    for n, w in dict(xt=512, wt=2048, vt=512, ebt=2048, trict=512, cht=1024, selt=512, d8t=512, ut=1024, wwt=512,
+                     x2t=512, yt=512, it=512, zt=512, mt=512, ht=512, hxt=512, y2t=512, ott=1024,
+                     roww=256, io=256, row16=128).items():
+        sb(n, w, "bfloat16")
+    for n, w in dict(mp=264, neg=256, br=96, tri=96, bb=192, ge=96, gt=96, cs=96, junk=256, idx=1, e9=16, d8=8, d48=8,
+                     offr=1, pm=1, om=1, stand=1, pay=8, y8=8, zer8=8, pcol=1, pm16=1, p32=1, ph16=1, init=1, ord8=8,
+                     basei=8, base=8, base2=8, fl=8, a2=2, t96=128, id256=128, rr=36, z4=4, zs=1, adm=1, adm0=1, df=1,
+                     blk=1, mgv=1, mgc=1, dig=4, yd=32, maskc=8, ysb=128, inf8=8).items():
+        sb(n, w)
+    for n in ("ci", "xi"):
+        sb(n, 3, "int32")
+    for n, w in dict(offc=2, off16=16, l2=4, fl16=8).items():
+        sb(n, w, "uint16")
+    for n, w in dict(xw=256, alla=256, wq=512, vq=128, eq=512, tq=128, cq=256, selq=128, d8q=128, uq=256, wwq=128, x2q=128,
+                     yq=128, sb=256, lb=288, pk=192, mq=128, hq=128, hb=384, otq=256, y2q=128, gq=128).items():
+        sb(n + "c", w, "float8_e4m3fn_x4")
+        sb(n + "s", w, "uint8")
+    for i in range(8):
+        SCRATCH["ps%d" % i] = ("psum", [128, 512], "float32")
+
+
+_bufs()
+DMAS = ["ldx", "ldw", "ldv", "ownc", "owns", "stmg", "stoc", "st0", "st1", "st2", "st3", "sty"]
+SEMAPHORES = ["qv", "qs", "qt", "qg", "arra", "arrb", "arrc", "loca", "locb", "locc"] + DMAS
+
+
+def rank_program(g, core, T, topo):
+    r = T.rank_of(core)
+    if r is None:
+        return
+    eng = {"v": g.vector, "s": g.scalar, "t": g.tensor, "g": g, "y": g.sync}
+    count = {"v": 0, "s": 0, "t": 0, "g": 0}
+    waited, acc, last = {}, {}, {}
+
+    def W(name, a=0, b=None, step=1, p0=0, p1=128):
+        return (name, a, SCRATCH[name][1][1] if b is None else b, step, p0, p1)
+
+    def ap(v):
+        name, a, b, step, p0, p1 = v
+        return T[name][p0:p1, a:b] if step == 1 else T[name][p0:p1, a:b:step]
+
+    def meet(v, w):
+        if v[0][:2] == "ps":
+            return True
+        if v[4] >= w[5] or w[4] >= v[5] or v[1] >= w[2] or w[1] >= v[2]:
+            return False
+        return not (v[3] == w[3] and v[3] > 1 and (v[1] - w[1]) % v[3])
+
+    def order(q, reads, writes, sem, val):
+        need = {}
+        for views, wr in ((reads, False), (writes, True)):
+            for v in views:
+                for (o, owr, osem, oval, oq) in acc.get(v[0], ()):
+                    bank = v[0][:2] == "ps"
+                    if oq == q == "t" and bank:
+                        continue
+                    if not (wr or owr or (bank and oq != q)) or not meet(v, o):
+                        continue
+                    need[osem] = max(need.get(osem, 0), oval)
+        for s in sorted(need):
+            wait(q, s, need[s])
+        for views, wr in ((reads, False), (writes, True)):
+            for v in views:
+                acc.setdefault(v[0], []).append((v, wr, sem, val, q))
+
+    def wait(q, sem, val):
+        if waited.get((q, sem), 0) < val:
+            waited[(q, sem)] = val
+            eng[q].wait_ge(T.sem[sem], val)
+
+    def op(q, reads, writes, call):
+        count[q] += 1
+        sem = "q" + q
+        order(q, reads, writes, sem, count[q])
+        call().then_inc(T.sem[sem], 1)
+        last[sem] = count[q]
+
+    def dma(q, sem, out, in_, reads, writes):
+        order(q, reads, writes, sem, 16)
+        eng[q].dma_start(out, in_).then_inc(T.sem[sem], 16)
+        last[sem] = 16
+
+    def landed(sem, val, views):
+        for v in views:
+            acc.setdefault(v[0], []).append((v, True, sem, val, "net"))
+        last[sem] = val
+
+    def sc(x):
+        return ap(x) if isinstance(x, tuple) else x
+
+    def vs(*xs):
+        return [x for x in xs if isinstance(x, tuple)]
+
+    def fill(v, c):
+        op("v", [], [v], lambda: g.vector.memset(ap(v), c))
+
+    def ts(out, in0, s1, op0, s2=None, op1=None):
+        if op1 is None:
+            op("v", vs(in0, s1), [out], lambda: g.vector.tensor_scalar(ap(out), ap(in0), sc(s1), None, op0))
+        else:
+            op("v", vs(in0, s1, s2), [out], lambda: g.vector.tensor_scalar(ap(out), ap(in0), sc(s1), sc(s2), op0, op1))
+
+    def tt(out, a, b, o):
+        op("v", [a, b], [out], lambda: g.vector.tensor_tensor(ap(out), ap(a), ap(b), o))
+
+    def copy(out, a):
+        op("v", [a], [out], lambda: g.vector.tensor_copy(ap(out), ap(a)))
+
+    def red(out, a, o):
+        op("v", [a], [out], lambda: g.vector.tensor_reduce(ap(out), ap(a), AxisListType.X, o))
+
+    def scan(out, d0, d1, init, o0, o1):
+        op("v", vs(d0, d1, init), [out], lambda: g.vector.tensor_tensor_scan(ap(out), ap(d0), ap(d1), sc(init), o0, o1))
+
+    def turn(out, a):
+        op("v", [a], [out], lambda: g.vector.transpose(ap(out), ap(a)))
+
+    def act(out, a, f, scale=1.0):
+        op("s", [a], [out], lambda: g.scalar.activation(ap(out), ap(a), f, scale=scale))
+
+    def zero(n):
+        for k in range(0, SCRATCH[n][1][1], 512):
+            act(W(n, k, k + 512), W("zt"), AF.Copy)
+
+    def quant(q, a, b, tile, c=0):
+        n = b - a
+        oc, os_, t = W(q + "c", a, b), W(q + "s", a, b), W(tile, c, c + 4 * n)
+        op("v", [t], [oc, os_], lambda: g.vector.quantize_mx(ap(oc), ap(os_), ap(t)))
+
+    def mm(bank, st, a, mv, b, n, start=True, stop=True):
+        o = W("ps%d" % bank, 0, n)
+        l, ls, m, ms = W(st + "c", a, a + 128), W(st + "s", a, a + 128), W(mv + "c", b, b + n), W(mv + "s", b, b + n)
+        op("t", [l, ls, m, ms], [o], lambda: g.tensor.matmul_mx(ap(o), ap(l), ap(ls), ap(m), ap(ms), start, stop))
+
+    def pick(dst, a, src, w, off):
+        n = 16 * (off[2] - off[1])
+        oc, os_, ic, is_ = W(dst + "c", a, a + n), W(dst + "s", a, a + n), W(src + "c", 0, w), W(src + "s", 0, w)
+        op("v", [ic, off], [oc], lambda: g.vector.tensor_copy(ap(oc).bitcast(dt.uint32), ap(ic).bitcast(dt.uint32).indirect(ap(off))))
+        op("s", [is_, off], [os_], lambda: g.scalar.activation(ap(os_), ap(is_).indirect(ap(off)), AF.Copy))
+
+    def iota(out, pattern, base, cm):
+        if SCRATCH[out[0]][2] == "int32":
+            op("g", [], [out], lambda: g.iota(ap(out), pattern, base, cm))
+        else:
+            op("g", [], [out], lambda: g.iota(ap(out), pattern, base, cm, allow_small_or_imprecise_dtypes=True))
+
+    others = [(r + k) % N for k in range(1, N)]
+
+    def dst_id(d):
+        rid, pid = topo.addr(T.cores[d], core)
+        return DstId(rid=rid, pnc=pid)
+
+    def everyone(src, a, dst, b, n, arr, loc):
+        mask = topo.mask(core, T.cores[others[0]])
+        for d in others:
+            mask &= topo.mask(core, T.cores[d])
+        k = bin(mask).count("1")
+        for x in "cs":
+            s, o = W(src + x, a, a + n), W(dst + x, b, b + n)
+            order("g", [s], [], loc, 2 * k)
+            sv, ov = ap(s), ap(o)
+            if x == "c":
+                sv, ov = sv.bitcast(dt.uint8), ov.bitcast(dt.uint8)
+            g.remote_dma_fused([RemoteDMATransfer(dst_ids=[dst_id(d) for d in others], dma_engine_mask=mask,
+                                                  remote_sem=T.sem[arr], srcs=[sv], dsts=[ov for d in others])],
+                               local_sem=T.sem[loc])
+        last[loc] = 2 * k
+        return 2 * k * (N - 1)
+
+    dma("y", "ldx", T.xt[:], T.x[:], [], [W("xt")])
+    iota(W("ci", 0, 1), [[0, 1]], 0, 1)
+    iota(W("pcol"), [[0, 1]], 0, 1)
+    iota(W("basei"), [[16, 8]], 0, 0)
+    iota(W("io"), [[1, 256]], 0, 0)
+    iota(W("row16"), [[0, 8], [1, 16]], 0, 0)
+    fill(W("zt"), 0.0)
+    for n in ("wwt", "x2t", "yt", "it"):
+        zero(n)
+    ts(W("ci", 1, 2), W("ci", 0, 1), 15, OP.bitwise_and)
+    ts(W("ci", 2, 3), W("ci", 0, 1), 31, OP.bitwise_and)
+    copy(W("pm16"), W("ci", 1, 2))
+    copy(W("p32"), W("ci", 2, 3))
+    ts(W("base"), W("basei"), W("pm16"), OP.add)
+    tt(W("ph16"), W("pcol"), W("pm16"), OP.subtract)
+    copy(W("offc"), W("base", 0, 2))
+    fill(W("neg"), -BIG)
+    fill(W("mp", 0, 1), -BIG)
+    fill(W("bb"), -BIG)
+    fill(W("d8t"), 0.0)
+    fill(W("ut"), 0.0)
+    quant("xw", 0, 128, "xt")
+    n_a = everyone("xw", 0, "alla", A * r, A, "arra", "loca")
+    landed("arra", n_a, [W("alla" + x, A * d, A * d + A) for d in others for x in "cs"])
+    iota(W("roww"), [[0, 8], [1, 16], [0, 2]], -256, 0)
+    iota(W("ord8"), [[1, 2], [0, 4]], -256, 0)
+    pick("alla", A * r, "xw", 128, W("offc"))
+    for n in ("cht", "mt", "ht", "ott"):
+        zero(n)
+    fill(W("tri", 0, 32), BIG)
+    ts(W("tri", 32, 64), W("io", 0, 32), W("p32"), OP.is_gt, 2 * BIG, OP.mult)
+    ts(W("tri", 64, 96), W("io", 0, 32), W("p32"), OP.is_lt, 2 * BIG, OP.mult)
+    ts(W("tri", 32, 96), W("tri", 32, 96), -BIG, OP.add)
+    fill(W("trict"), 0.0)
+    ts(W("t96"), W("io", 0, 128), W("pcol"), OP.is_gt)
+    ts(W("id256"), W("io", 0, 128), W("pcol"), OP.is_equal, -256.0, OP.mult)
+    tt(W("trict", 0, 512, 4), W("t96"), W("id256"), OP.add)
+    quant("tq", 0, 128, "trict")
+    fill(W("init"), 0.0)
+    fill(W("init", 0, 1, 1, 0, A), 1000.0)
+    fill(W("zer8"), 0.0)
+    ts(W("inf8"), W("zer8"), W("pm16"), OP.add, 3.0, OP.min)
+    ts(W("off16", 1, 16, 2), W("inf8"), 128.0, OP.add)
+    m = N - r
+    fill(W("pay"), 1.0)
+    fill(W("pay", 0, 8, 4), -16.0 * m)
+    fill(W("pay", 1, 8, 4), -4.0 * m)
+    fill(W("ebt"), 0.0)
+    for i in range(4):
+        ts(W("ebt", 512 * i + i, 512 * i + 512, 4), W("io", 0, 128), W("pcol"), OP.is_equal)
+    quant("eq", 0, 512, "ebt")
+    for h in range(2):
+        for t in range(3):
+            ts(W("cht", 512 * h + t, 512 * h + 512, 4), W("row16"), float((A * r) % 128 + 16 * h), OP.add, W("pcol"), OP.is_equal)
+    quant("cq", 0, 256, "cht")
+    quant("lb", NONE, NONE + 128, "zt")
+    quant("pk", 64, 192, "zt")
+    fill(W("rr"), 0.0)
+
+    wait("y", "arra", n_a)
+    dma("y", "ldw", T.wt[:], T.w[:], [], [W("wt")])
+    dma("y", "ldv", T.vt[:], T.v[:], [], [W("vt")])
+    mm(0, "xw", 0, "alla", 0, 256)
+    b = W("mp", 256, 257)
+    scan(W("mp", 1, 257), W("ps0", 0, 256), W("neg"), -BIG, OP.max, OP.max)
+    op("s", [W("mp", 1, 257), b], [W("junk"), W("idx")],
+       lambda: g.scalar.activation(T.junk[:], T.mp[:, 1:257], AF.Sign, bias=ap(b), scale=-1.0, accum_out=T.idx[:]))
+    ts(W("br"), W("tri"), b, OP.min)
+    ts(W("e9", 0, 9), W("mp", 0, 257, 32), b, OP.is_lt)
+    turn(W("bb", 64, 128), W("br", 32, 96))
+    for me, him, at in ((1, 2, 128), (1, 3, 160), (2, 1, 32), (2, 3, 128), (3, 1, 32), (3, 2, 0)):
+        turn(W("bb", at, at + 32, 1, 32 * me, 32 * me + 32), W("br", 0, 32, 1, 32 * him, 32 * him + 32))
+    tt(W("d8"), W("e9", 0, 8), W("e9", 1, 9), OP.subtract)
+    ts(W("ge"), W("bb", 0, 96), b, OP.is_ge)
+    ts(W("gt"), W("bb", 96, 192), b, OP.is_gt)
+    ts(W("d48"), W("d8"), float(KM), OP.mult)
+    scan(W("cs"), W("ge"), W("gt"), W("init"), OP.add, OP.add)
+    c = W("cs", 95, 96)
+    ts(W("d8t", 0, 32, 4), W("d48"), c, OP.is_gt)
+    ts(W("offr"), c, float(KM), OP.is_lt)
+    quant("d8q", 0, 128, "d8t")
+    mm(1, "tq", 0, "d8q", 0, 128)
+    ts(W("ut", 0, 1024, 4), W("io"), W("idx"), OP.is_equal, W("offr"), OP.mult)
+    quant("uq", 0, 256, "ut")
+    mm(2, "tq", 0, "uq", 0, 256)
+    red(W("pm"), W("ps1", 0, 8), OP.min)
+    ts(W("x2t", 0, 32, 4), W("d8"), W("ph16"), OP.mult)
+    ts(W("x2t", 2, 32, 4), W("d8"), W("pm16"), OP.mult)
+    ts(W("wwt", 0, 512, 2), W("roww"), W("pm"), OP.is_equal)
+    ts(W("stand"), W("pm"), -256.0 + CAPP, OP.is_lt)
+    ts(W("pay", 2, 8, 4), W("zer8", 0, 2), W("pm"), OP.add, 256.0, OP.add)
+    red(W("om"), W("ps2", 0, 256), OP.min)
+    quant("wwq", 0, 128, "wwt")
+    quant("x2q", 0, 128, "x2t")
+    mm(3, "wwq", 0, "x2q", 0, 128)
+    ts(W("y8"), W("ord8"), W("om"), OP.is_equal, W("stand"), OP.mult)
+    tt(W("yt", 0, 32, 4), W("y8"), W("pay"), OP.mult)
+    quant("yq", 0, 128, "yt")
+    mm(0, "uq", 0, "yq", 0, 128)
+    mm(1, "uq", 128, "yq", 0, 128)
+    copy(W("off16", 0, 16, 2), W("ps3", 0, 8))
+    copy(W("it", 0, 8), W("ps0", 0, 8))
+    act(W("it", 8, 16), W("ps1", 0, 8), AF.Copy)
+    quant("xw", 128, 256, "it")
+    pick("sb", 0, "xw", 256, W("off16"))
+    for x in "cs":
+        tr = []
+        for k, d in enumerate(others):
+            s, o = W("sb" + x, 32 * d, 32 * d + RUN), W("lb" + x, RUN * r, RUN * r + RUN)
+            order("g", [s], [], "locb", 2 * (N - 1))
+            e = topo.engines(core, T.cores[d])
+            sv, ov = ap(s), ap(o)
+            if x == "c":
+                sv, ov = sv.bitcast(dt.uint8), ov.bitcast(dt.uint8)
+            tr.append(RemoteDMATransfer(dst_ids=[dst_id(d)], dma_engine_mask=1 << e[(k + (x == "s")) % len(e)],
+                                        remote_sem=T.sem.arrb, srcs=[sv], dsts=[ov]))
+        g.remote_dma_fused(tr, local_sem=T.sem.locb)
+    last["locb"] = 2 * (N - 1)
+    landed("arrb", 2 * (N - 1), [W("lb" + x, RUN * d, RUN * d + RUN) for d in others for x in "cs"])
+    sc_, ss_ = W("sbc", 32 * r, 32 * r + RUN), W("sbs", 32 * r, 32 * r + RUN)
+    lc_, ls_ = W("lbc", RUN * r, RUN * r + RUN), W("lbs", RUN * r, RUN * r + RUN)
+    dma("y", "ownc", ap(lc_).bitcast(dt.uint8), ap(sc_).bitcast(dt.uint8), [sc_], [lc_])
+    dma("s", "owns", ap(ls_), ap(ss_), [ss_], [ls_])
+    for h in range(2):
+        mm(2 + h, "uq", 128 * h, "eq", 0, 128)
+    for h in range(2):
+        act(W("ott", 512 * h + 3, 512 * h + 512, 4), W("ps%d" % (2 + h), 0, 128), AF.Copy)
+    quant("wq", 0, 512, "wt")
+    for i in range(4):
+        mm(4 + i, "wq", 128 * i, "xw", 0, 128)
+    for i in range(4):
+        act(W("hxt", i, 512, 4), W("ps%d" % (4 + i), 0, 128), AF.Relu, 0.0625)
+    quant("otq", 0, 256, "ott")
+    quant("hb", 0, 128, "hxt")
+    for i in range(4):
+        mm(4 + i, "eq", 128 * i, "xw", 0, 128, True, False)
+
+    for h in range(2):
+        mm(h, "cq", 128 * h, "lb", 0, RUN * N)
+    for h in range(2):
+        mm(2 + h, "otq", 128 * h, "lb", 0, RUN * N)
+    o1 = CAPP + 2 * (r // 4)
+
+    def ent(h, o):
+        return W("ps%d" % h, o1 + o, RUN * N, RUN)
+    for h in range(2):
+        scan(W("rr", 9 * h + 1, 9 * h + 9), ent(h, 0), W("zer8"), 0.0, OP.min, OP.min)
+    for h in range(2):
+        tt(W("rr", 19 + 9 * h, 27 + 9 * h), ent(h, 0), W("rr", 9 * h, 9 * h + 8), OP.max)
+    for h in range(2):
+        scan(W("yd", 8 * h, 8 * h + 8), W("rr", 19 + 9 * h, 27 + 9 * h), ent(h, 1), 0.0, OP.min, OP.min)
+    ts(W("l2", 0, 2), W("rr", 8, 18, 9), float(NONE), OP.add)
+    ts(W("l2", 2, 4), W("yd", 7, 16, 8), float(NONE), OP.add)
+    pick("pk", 0, "lb", 288, W("l2"))
+    for i in range(4):
+        mm(4 + i, "eq", 128 * i, "pk", 0, 128, False, False)
+        mm(4 + i, "eq", 128 * i, "pk", 32, 128, False, True)
+    if r:
+        for h in range(2):
+            for o in range(2):
+                red(W("z4", 2 * h + o, 2 * h + o + 1), W("ps%d" % (2 + h), CAPP + 2 * h + o, RUN * r, RUN), OP.add)
+    for i in range(4):
+        o, p = W("mt", i, 128, 4), W("ps%d" % (4 + i), 0, 32)
+        if i % 2:
+            ts(o, p, 0.5, OP.mult)
+        else:
+            act(o, p, AF.Copy, 0.5)
+    quant("mq", 0, 128, "mt")
+    for i in range(4):
+        mm(i, "wq", 128 * i, "mq", 0, 128)
+    for i in range(4):
+        o, p = W("ht", i, 128, 4), W("ps%d" % i, 0, 32)
+        if i % 2:
+            ts(o, p, 0.0, OP.max, 0.0625, OP.mult)
+        else:
+            act(o, p, AF.Relu, 0.0625)
+    quant("hq", 0, 128, "ht")
+    n_c = everyone("hq", 0, "hb", 128 + A * r, A, "arrc", "locc")
+    landed("arrc", n_c, [W("hb" + x, 128 + A * d, 128 + A * d + A) for d in others for x in "cs"])
+    pick("hb", 128 + A * r, "hq", 128, W("offc"))
+    if r:
+        red(W("zs"), W("z4"), OP.add)
+        ts(W("adm0"), W("zs"), W("om"), OP.add, -254.0, OP.is_lt)
+    else:
+        ts(W("adm0"), W("om"), -254.0, OP.is_lt)
+    copy(W("xi", 0, 1), W("idx"))
+    ts(W("selt", 0, 512, 4), W("row16"), W("pm16"), OP.is_equal)
+    tt(W("adm"), W("adm0"), W("stand"), OP.mult)
+    ts(W("xi", 1, 2), W("xi", 0, 1), 15, OP.bitwise_and)
+    ts(W("xi", 2, 3), W("xi", 0, 1), 5, OP.arith_shift_right)
+    for t in range(1, 4):
+        ts(W("selt", t, 512, 4), W("row16"), W("pm16"), OP.is_equal)
+    copy(W("dig", 1, 2), W("xi", 1, 2))
+    copy(W("df"), W("xi", 2, 3))
+    quant("selq", 0, 128, "selt")
+    ts(W("maskc"), W("basei"), W("ph16"), OP.is_equal, W("adm"), OP.mult)
+    tt(W("dig", 0, 1), W("idx"), W("dig", 1, 2), OP.subtract)
+    ts(W("dig", 2, 3), W("ph16"), -1.0, OP.mult, 128.0, OP.add)
+    ts(W("dig", 3, 4), W("pm16"), -1.0, OP.mult)
+    fill(W("y2t"), 0.0)
+    for t in range(4):
+        ts(W("y2t", t, 32, 4), W("maskc"), W("dig", t, t + 1), OP.mult)
+    quant("y2q", 0, 128, "y2t")
+    mm(4, "selq", 0, "y2q", 0, 128)
+    copy(W("base2"), W("base"))
+    ts(W("a2"), W("rr", 8, 18, 9), 0.0, OP.is_lt, float(128 + A * r), OP.mult)
+    ts(W("mgv"), W("df"), 96.0, OP.mult, W("idx"), OP.add)
+    tt(W("base2", 0, 2), W("base", 0, 2), W("a2"), OP.add)
+    tt(W("fl"), W("ps4", 0, 8), W("base2"), OP.add)
+    ts(W("blk"), W("mgv"), 1.0, OP.add, W("adm"), OP.mult)
+    copy(W("fl16"), W("fl"))
+    ts(W("mgc"), W("blk"), -1.0, OP.add)
+    dma("y", "stmg", T.mg[:], T.mgc[:], [W("mgc")], [])
+    quant("vq", 0, 128, "vt")
+
+    pick("gq", 0, "hb", 384, W("fl16"))
+    dma("y", "stoc", T.oc[:], T.gqc[:].bitcast(dt.uint8), [W("gqc")], [])
+    for k in range(4):
+        v = W("gqs", 0, 128, 1, 32 * k, 32 * k + 4)
+        dma("s", "st%d" % k, T.osc[4 * k:4 * k + 4, :], ap(v), [v], [])
+    mm(5, "vq", 0, "gq", 0, 128)
+    copy(W("ysb"), W("ps5", 0, 128))
+    dma("y", "sty", T.y[:], T.ysb[:], [W("ysb")], [])
+    for s in sorted(last):
+        wait("g", s, last[s])

@@ -12,21 +12,22 @@ SCRATCH = {}
 def _bufs():
     def sb(n, w, d="float32"):
         SCRATCH[n] = ("sbuf", [128, w], d)
-    for n, w in dict(xt=512, wt=2048, vt=512, ebt=2048, trict=512, cht=1024, selt=512, d8t=512, ut=1024, wwt=512,
+    for n, w in dict(xa=512, xt=512, wt=2048, vt=512, ebt=2048, trict=512, cht=1024, selt=512, d8t=512, ut=1024, wwt=512,
                      x2t=512, yt=512, it=512, zt=512, mt=512, ht=512, hxt=512, y2t=512, ott=1024,
                      roww=256, io=256, row16=128).items():
         sb(n, w, "bfloat16")
-    for n, w in dict(mp=264, neg=256, br=96, tri=96, bb=192, ge=96, gt=96, cs=96, junk=256, idx=1, e9=16, d8=8, d48=8,
-                     offr=1, pm=1, om=1, stand=1, pay=8, y8=8, zer8=8, pcol=1, pm16=1, p32=1, ph16=1, init=1, ord8=8,
-                     basei=8, base=8, base2=8, fl=8, a2=2, t96=128, id256=128, rr=36, z4=4, zs=1, adm=1, adm0=1, df=1,
-                     blk=1, mgv=1, mgc=1, dig=4, yd=32, maskc=8, ysb=128, inf8=8).items():
+    for n, w in dict(mp=264, neg=256, br=96, tri=96, bb=192, ge=96, gt=96, cs=96, junk=256, idx=2, e9=16, d8=8, d48=8,
+                     pm=2, om=3, pay=8, pays=8, y8=8, zer8=8, pc=4, init=1, ord8=8,
+                     basei=8, base=8, base2=8, fl=8, a2=2, t96=128, id256=128, rr=36, z4=6, adm=1, df=1,
+                     mgv=3, dig=4, yd=32, maskc=8, ysb=128, inf8=8).items():
         sb(n, w)
     for n in ("ci", "xi"):
         sb(n, 3, "int32")
     for n, w in dict(offc=2, off16=16, l2=4, fl16=8).items():
         sb(n, w, "uint16")
-    for n, w in dict(xw=256, alla=256, wq=512, vq=128, eq=512, tq=128, cq=256, selq=128, d8q=128, uq=256, wwq=128, x2q=128,
-                     yq=128, sb=256, lb=288, pk=192, mq=128, hq=128, hb=384, otq=256, y2q=128, gq=128).items():
+    for n, w in dict(qa=128, xw=256, alla=256, wq=512, vq=128, eq=512, tq=128, cq=256, selq=128, d8q=128, uq=256, wwq=128,
+                     x2q=128, yq=128, sb=256, lb=288, pk=160, pk2=160, mq=128, hq=128, hb=384, otq=256, y2q=128,
+                     gq=128).items():
         sb(n + "c", w, "float8_e4m3fn_x4")
         sb(n + "s", w, "uint8")
     for i in range(8):
@@ -34,7 +35,7 @@ def _bufs():
 
 
 _bufs()
-DMAS = ["ldx", "ldw", "ldv", "ownc", "owns", "stmg", "stoc", "st0", "st1", "st2", "st3", "sty"]
+DMAS = ["lda", "ldx", "ldw", "ldv", "ownc", "owns", "stmg", "stoc", "st0", "st1", "st2", "st3", "sty"]
 SEMAPHORES = ["qv", "qs", "qt", "qg", "arra", "arrb", "arrc", "loca", "locb", "locc"] + DMAS
 
 
@@ -132,6 +133,12 @@ def rank_program(g, core, T, topo):
     def act(out, a, f, scale=1.0):
         op("s", [a], [out], lambda: g.scalar.activation(ap(out), ap(a), f, scale=scale))
 
+    def acol(out, a, col):
+        op("s", [a, col], [out], lambda: g.scalar.activation(ap(out), ap(a), AF.Identity, scale=ap(col)))
+
+    def asum(out, a, total):
+        op("s", [a], [out, total], lambda: g.scalar.activation(ap(out), ap(a), AF.Relu, scale=-1.0, accum_out=ap(total)))
+
     def zero(n):
         for k in range(0, SCRATCH[n][1][1], 512):
             act(W(n, k, k + 512), W("zt"), AF.Copy)
@@ -159,125 +166,129 @@ def rank_program(g, core, T, topo):
             op("g", [], [out], lambda: g.iota(ap(out), pattern, base, cm, allow_small_or_imprecise_dtypes=True))
 
     others = [(r + k) % N for k in range(1, N)]
+    away = [e for e in range(16) if all(e in topo.engines(core, T.cores[d]) for d in others)]
+
+    def bits(es):
+        return sum(1 << e for e in es)
 
     def dst_id(d):
         rid, pid = topo.addr(T.cores[d], core)
         return DstId(rid=rid, pnc=pid)
 
-    def everyone(src, a, dst, b, n, arr, loc):
-        mask = topo.mask(core, T.cores[others[0]])
-        for d in others:
-            mask &= topo.mask(core, T.cores[d])
-        k = bin(mask).count("1")
-        for x in "cs":
-            s, o = W(src + x, a, a + n), W(dst + x, b, b + n)
-            order("g", [s], [], loc, 2 * k)
+    def send(x, parts, arr, loc):
+        tr = []
+        for ds, s, o, es in parts:
+            order("g", [s], [], loc, 0)
             sv, ov = ap(s), ap(o)
             if x == "c":
                 sv, ov = sv.bitcast(dt.uint8), ov.bitcast(dt.uint8)
-            g.remote_dma_fused([RemoteDMATransfer(dst_ids=[dst_id(d) for d in others], dma_engine_mask=mask,
-                                                  remote_sem=T.sem[arr], srcs=[sv], dsts=[ov for d in others])],
-                               local_sem=T.sem[loc])
-        last[loc] = 2 * k
-        return 2 * k * (N - 1)
+            tr.append(RemoteDMATransfer(dst_ids=[dst_id(d) for d in ds], dma_engine_mask=bits(es), remote_sem=T.sem[arr],
+                                        srcs=[sv], dsts=[ov for d in ds]))
+        g.remote_dma_fused(tr, local_sem=T.sem[loc])
+        last[loc] = last.get(loc, 0) + sum(len(p[3]) for p in parts)
 
+    def everyone(src, a, dst, b, n, arr, loc):
+        for x in "cs":
+            send(x, [(others, W(src + x, a, a + n), W(dst + x, b, b + n), away)], arr, loc)
+        return 2 * len(away) * (N - 1)
+
+    dma("y", "lda", T.xa[:, 0:4 * A], T.x[:, 0:4 * A], [], [W("xa", 0, 4 * A)])
     dma("y", "ldx", T.xt[:], T.x[:], [], [W("xt")])
+    PCOL, PM16, P32, PH16 = [W("pc", i, i + 1) for i in range(4)]
     iota(W("ci", 0, 1), [[0, 1]], 0, 1)
-    iota(W("pcol"), [[0, 1]], 0, 1)
+    iota(PCOL, [[0, 1]], 0, 1)
     iota(W("basei"), [[16, 8]], 0, 0)
     iota(W("io"), [[1, 256]], 0, 0)
     iota(W("row16"), [[0, 8], [1, 16]], 0, 0)
     fill(W("zt"), 0.0)
+    fill(W("xa", 4 * A, 512), 0.0)
     for n in ("wwt", "x2t", "yt", "it"):
         zero(n)
     ts(W("ci", 1, 2), W("ci", 0, 1), 15, OP.bitwise_and)
     ts(W("ci", 2, 3), W("ci", 0, 1), 31, OP.bitwise_and)
-    copy(W("pm16"), W("ci", 1, 2))
-    copy(W("p32"), W("ci", 2, 3))
-    ts(W("base"), W("basei"), W("pm16"), OP.add)
-    tt(W("ph16"), W("pcol"), W("pm16"), OP.subtract)
+    copy(PM16, W("ci", 1, 2))
+    copy(P32, W("ci", 2, 3))
+    ts(W("base"), W("basei"), PM16, OP.add)
+    tt(PH16, PCOL, PM16, OP.subtract)
     copy(W("offc"), W("base", 0, 2))
     fill(W("neg"), -BIG)
     fill(W("mp", 0, 1), -BIG)
     fill(W("bb"), -BIG)
+    quant("qa", 0, 128, "xa")
+    n_a = everyone("qa", 0, "alla", A * r, A, "arra", "loca")
+    landed("arra", n_a, [W("alla" + x, A * d, A * d + A) for d in others for x in "cs"])
+    wait("y", "loca", last["loca"])
+    dma("y", "ldw", T.wt[:], T.w[:], [], [W("wt")])
+    dma("y", "ldv", T.vt[:], T.v[:], [], [W("vt")])
+    iota(W("roww"), [[0, 8], [1, 16], [0, 2]], -256, 0)
+    iota(W("ord8"), [[-1, 2], [0, 4]], 256, 0)
+    pick("alla", A * r, "qa", 128, W("offc"))
+    quant("xw", 0, 128, "xt")
     fill(W("d8t"), 0.0)
     fill(W("ut"), 0.0)
-    quant("xw", 0, 128, "xt")
-    n_a = everyone("xw", 0, "alla", A * r, A, "arra", "loca")
-    landed("arra", n_a, [W("alla" + x, A * d, A * d + A) for d in others for x in "cs"])
-    iota(W("roww"), [[0, 8], [1, 16], [0, 2]], -256, 0)
-    iota(W("ord8"), [[1, 2], [0, 4]], -256, 0)
-    pick("alla", A * r, "xw", 128, W("offc"))
-    for n in ("cht", "mt", "ht", "ott"):
+    for n in ("ebt", "ott"):
         zero(n)
     fill(W("tri", 0, 32), BIG)
-    ts(W("tri", 32, 64), W("io", 0, 32), W("p32"), OP.is_gt, 2 * BIG, OP.mult)
-    ts(W("tri", 64, 96), W("io", 0, 32), W("p32"), OP.is_lt, 2 * BIG, OP.mult)
+    ts(W("tri", 32, 64), W("io", 0, 32), P32, OP.is_gt, 2 * BIG, OP.mult)
+    ts(W("tri", 64, 96), W("io", 0, 32), P32, OP.is_lt, 2 * BIG, OP.mult)
     ts(W("tri", 32, 96), W("tri", 32, 96), -BIG, OP.add)
     fill(W("trict"), 0.0)
-    ts(W("t96"), W("io", 0, 128), W("pcol"), OP.is_gt)
-    ts(W("id256"), W("io", 0, 128), W("pcol"), OP.is_equal, -256.0, OP.mult)
+    ts(W("t96"), W("io", 0, 128), PCOL, OP.is_gt)
+    ts(W("id256"), W("io", 0, 128), PCOL, OP.is_equal, -256.0, OP.mult)
     tt(W("trict", 0, 512, 4), W("t96"), W("id256"), OP.add)
     quant("tq", 0, 128, "trict")
     fill(W("init"), 0.0)
     fill(W("init", 0, 1, 1, 0, A), 1000.0)
     fill(W("zer8"), 0.0)
-    ts(W("inf8"), W("zer8"), W("pm16"), OP.add, 3.0, OP.min)
+    ts(W("inf8"), W("zer8"), PM16, OP.add, 3.0, OP.min)
     ts(W("off16", 1, 16, 2), W("inf8"), 128.0, OP.add)
     m = N - r
     fill(W("pay"), 1.0)
     fill(W("pay", 0, 8, 4), -16.0 * m)
     fill(W("pay", 1, 8, 4), -4.0 * m)
-    fill(W("ebt"), 0.0)
     for i in range(4):
-        ts(W("ebt", 512 * i + i, 512 * i + 512, 4), W("io", 0, 128), W("pcol"), OP.is_equal)
+        ts(W("ebt", 512 * i + i, 512 * i + 512, 4), W("io", 0, 128), PCOL, OP.is_equal)
     quant("eq", 0, 512, "ebt")
-    for h in range(2):
-        for t in range(3):
-            ts(W("cht", 512 * h + t, 512 * h + 512, 4), W("row16"), float((A * r) % 128 + 16 * h), OP.add, W("pcol"), OP.is_equal)
-    quant("cq", 0, 256, "cht")
-    quant("lb", NONE, NONE + 128, "zt")
-    quant("pk", 64, 192, "zt")
-    fill(W("rr"), 0.0)
 
-    wait("y", "arra", n_a)
-    dma("y", "ldw", T.wt[:], T.w[:], [], [W("wt")])
-    dma("y", "ldv", T.vt[:], T.v[:], [], [W("vt")])
     mm(0, "xw", 0, "alla", 0, 256)
     b = W("mp", 256, 257)
     scan(W("mp", 1, 257), W("ps0", 0, 256), W("neg"), -BIG, OP.max, OP.max)
-    op("s", [W("mp", 1, 257), b], [W("junk"), W("idx")],
-       lambda: g.scalar.activation(T.junk[:], T.mp[:, 1:257], AF.Sign, bias=ap(b), scale=-1.0, accum_out=T.idx[:]))
+    idx, offr, pm, stand = W("idx", 0, 1), W("idx", 1, 2), W("pm", 0, 1), W("pm", 1, 2)
+    op("s", [W("mp", 1, 257), b], [W("junk"), idx],
+       lambda: g.scalar.activation(T.junk[:], T.mp[:, 1:257], AF.Sign, bias=ap(b), scale=-1.0, accum_out=ap(idx)))
     ts(W("br"), W("tri"), b, OP.min)
     ts(W("e9", 0, 9), W("mp", 0, 257, 32), b, OP.is_lt)
     turn(W("bb", 64, 128), W("br", 32, 96))
     for me, him, at in ((1, 2, 128), (1, 3, 160), (2, 1, 32), (2, 3, 128), (3, 1, 32), (3, 2, 0)):
         turn(W("bb", at, at + 32, 1, 32 * me, 32 * me + 32), W("br", 0, 32, 1, 32 * him, 32 * him + 32))
     tt(W("d8"), W("e9", 0, 8), W("e9", 1, 9), OP.subtract)
+    act(W("d48"), W("d8"), AF.Copy, float(KM))
+    acol(W("x2t", 0, 32, 4), W("d8"), PH16)
+    acol(W("x2t", 2, 32, 4), W("d8"), PM16)
     ts(W("ge"), W("bb", 0, 96), b, OP.is_ge)
     ts(W("gt"), W("bb", 96, 192), b, OP.is_gt)
-    ts(W("d48"), W("d8"), float(KM), OP.mult)
     scan(W("cs"), W("ge"), W("gt"), W("init"), OP.add, OP.add)
     c = W("cs", 95, 96)
     ts(W("d8t", 0, 32, 4), W("d48"), c, OP.is_gt)
-    ts(W("offr"), c, float(KM), OP.is_lt)
+    ts(offr, c, float(KM), OP.is_lt)
     quant("d8q", 0, 128, "d8t")
     mm(1, "tq", 0, "d8q", 0, 128)
-    ts(W("ut", 0, 1024, 4), W("io"), W("idx"), OP.is_equal, W("offr"), OP.mult)
-    quant("uq", 0, 256, "ut")
-    mm(2, "tq", 0, "uq", 0, 256)
-    red(W("pm"), W("ps1", 0, 8), OP.min)
-    ts(W("x2t", 0, 32, 4), W("d8"), W("ph16"), OP.mult)
-    ts(W("x2t", 2, 32, 4), W("d8"), W("pm16"), OP.mult)
-    ts(W("wwt", 0, 512, 2), W("roww"), W("pm"), OP.is_equal)
-    ts(W("stand"), W("pm"), -256.0 + CAPP, OP.is_lt)
-    ts(W("pay", 2, 8, 4), W("zer8", 0, 2), W("pm"), OP.add, 256.0, OP.add)
-    red(W("om"), W("ps2", 0, 256), OP.min)
+    for h in range(2):
+        ts(W("ut", 512 * h, 512 * h + 512, 4), W("io", 128 * h, 128 * h + 128), idx, OP.is_equal, offr, OP.mult)
+        quant("uq", 128 * h, 128 * h + 128, "ut", 512 * h)
+        mm(2 + 2 * h, "tq", 0, "uq", 128 * h, 128)
+    red(pm, W("ps1", 0, 8), OP.min)
+    ts(W("wwt", 0, 512, 2), W("roww"), pm, OP.is_equal)
+    ts(stand, pm, -256.0 + CAPP, OP.is_lt)
+    ts(W("pay", 2, 8, 4), W("zer8", 0, 2), pm, OP.add, 256.0, OP.add)
     quant("wwq", 0, 128, "wwt")
     quant("x2q", 0, 128, "x2t")
     mm(3, "wwq", 0, "x2q", 0, 128)
-    ts(W("y8"), W("ord8"), W("om"), OP.is_equal, W("stand"), OP.mult)
-    tt(W("yt", 0, 32, 4), W("y8"), W("pay"), OP.mult)
+    ts(W("pays"), W("pay"), stand, OP.mult)
+    for h in range(2):
+        asum(W("junk", 0, 128), W("ps%d" % (2 + 2 * h), 0, 128), W("om", 1 + h, 2 + h))
+    ts(W("y8"), W("ord8"), W("om", 1, 2), OP.subtract, W("om", 2, 3), OP.is_equal)
+    tt(W("yt", 0, 32, 4), W("y8"), W("pays"), OP.mult)
     quant("yq", 0, 128, "yt")
     mm(0, "uq", 0, "yq", 0, 128)
     mm(1, "uq", 128, "yq", 0, 128)
@@ -286,20 +297,15 @@ def rank_program(g, core, T, topo):
     act(W("it", 8, 16), W("ps1", 0, 8), AF.Copy)
     quant("xw", 128, 256, "it")
     pick("sb", 0, "xw", 256, W("off16"))
+    e = away
+    groups = {"c": ((0, e[0:2]), (1, e[2:4]), (2, e[4:6]), (3, e[6:8]), (4, e[0:2]), (5, e[2:4]), (6, e[4:8])),
+              "s": ((0, e[0:2]), (1, e[2:4]), (2, e[4:6]), (3, e[6:8]), (4, e[4:6]), (5, e[6:8]), (6, e[0:4]))}
     for x in "cs":
-        tr = []
-        for k, d in enumerate(others):
-            s, o = W("sb" + x, 32 * d, 32 * d + RUN), W("lb" + x, RUN * r, RUN * r + RUN)
-            order("g", [s], [], "locb", 2 * (N - 1))
-            e = topo.engines(core, T.cores[d])
-            sv, ov = ap(s), ap(o)
-            if x == "c":
-                sv, ov = sv.bitcast(dt.uint8), ov.bitcast(dt.uint8)
-            tr.append(RemoteDMATransfer(dst_ids=[dst_id(d)], dma_engine_mask=1 << e[(k + (x == "s")) % len(e)],
-                                        remote_sem=T.sem.arrb, srcs=[sv], dsts=[ov]))
-        g.remote_dma_fused(tr, local_sem=T.sem.locb)
-    last["locb"] = 2 * (N - 1)
-    landed("arrb", 2 * (N - 1), [W("lb" + x, RUN * d, RUN * d + RUN) for d in others for x in "cs"])
+        for part in (groups[x][:4], groups[x][4:]):
+            send(x, [([others[k]], W("sb" + x, 32 * others[k], 32 * others[k] + RUN), W("lb" + x, RUN * r, RUN * r + RUN), es)
+                     for k, es in part], "arrb", "locb")
+    n_b = sum(len(es) for x in "cs" for k, es in groups[x])
+    landed("arrb", n_b, [W("lb" + x, RUN * d, RUN * d + RUN) for d in others for x in "cs"])
     sc_, ss_ = W("sbc", 32 * r, 32 * r + RUN), W("sbs", 32 * r, 32 * r + RUN)
     lc_, ls_ = W("lbc", RUN * r, RUN * r + RUN), W("lbs", RUN * r, RUN * r + RUN)
     dma("y", "ownc", ap(lc_).bitcast(dt.uint8), ap(sc_).bitcast(dt.uint8), [sc_], [lc_])
@@ -314,9 +320,20 @@ def rank_program(g, core, T, topo):
     for i in range(4):
         act(W("hxt", i, 512, 4), W("ps%d" % (4 + i), 0, 128), AF.Relu, 0.0625)
     quant("otq", 0, 256, "ott")
+    ts(W("om", 0, 1), W("om", 1, 2), -1.0, OP.mult, W("om", 2, 3), OP.subtract)
     quant("hb", 0, 128, "hxt")
     for i in range(4):
         mm(4 + i, "eq", 128 * i, "xw", 0, 128, True, False)
+    for n in ("cht", "mt", "ht"):
+        zero(n)
+    fill(W("rr"), 0.0)
+    quant("lb", NONE, NONE + 128, "zt")
+    quant("pk", 32, 160, "zt")
+    quant("pk2", 32, 160, "zt")
+    for h in range(2):
+        for t in range(3):
+            ts(W("cht", 512 * h + t, 512 * h + 512, 4), W("row16"), float((A * r) % 128 + 16 * h), OP.add, PCOL, OP.is_equal)
+    quant("cq", 0, 256, "cht")
 
     for h in range(2):
         mm(h, "cq", 128 * h, "lb", 0, RUN * N)
@@ -328,16 +345,18 @@ def rank_program(g, core, T, topo):
         return W("ps%d" % h, o1 + o, RUN * N, RUN)
     for h in range(2):
         scan(W("rr", 9 * h + 1, 9 * h + 9), ent(h, 0), W("zer8"), 0.0, OP.min, OP.min)
+    ts(W("l2", 0, 2), W("rr", 8, 18, 9), float(NONE), OP.add)
+    pick("pk", 0, "lb", 288, W("l2", 0, 2))
     for h in range(2):
         tt(W("rr", 19 + 9 * h, 27 + 9 * h), ent(h, 0), W("rr", 9 * h, 9 * h + 8), OP.max)
     for h in range(2):
         scan(W("yd", 8 * h, 8 * h + 8), W("rr", 19 + 9 * h, 27 + 9 * h), ent(h, 1), 0.0, OP.min, OP.min)
-    ts(W("l2", 0, 2), W("rr", 8, 18, 9), float(NONE), OP.add)
     ts(W("l2", 2, 4), W("yd", 7, 16, 8), float(NONE), OP.add)
-    pick("pk", 0, "lb", 288, W("l2"))
+    pick("pk2", 0, "lb", 288, W("l2", 2, 4))
     for i in range(4):
         mm(4 + i, "eq", 128 * i, "pk", 0, 128, False, False)
-        mm(4 + i, "eq", 128 * i, "pk", 32, 128, False, True)
+    for i in range(4):
+        mm(4 + i, "eq", 128 * i, "pk2", 0, 128, False, True)
     if r:
         for h in range(2):
             for o in range(2):
@@ -362,24 +381,24 @@ def rank_program(g, core, T, topo):
     landed("arrc", n_c, [W("hb" + x, 128 + A * d, 128 + A * d + A) for d in others for x in "cs"])
     pick("hb", 128 + A * r, "hq", 128, W("offc"))
     if r:
-        red(W("zs"), W("z4"), OP.add)
-        ts(W("adm0"), W("zs"), W("om"), OP.add, -254.0, OP.is_lt)
+        red(W("z4", 4, 5), W("z4", 0, 4), OP.add)
+        ts(W("z4", 5, 6), W("z4", 4, 5), W("om", 0, 1), OP.add, -254.0, OP.is_lt)
     else:
-        ts(W("adm0"), W("om"), -254.0, OP.is_lt)
-    copy(W("xi", 0, 1), W("idx"))
-    ts(W("selt", 0, 512, 4), W("row16"), W("pm16"), OP.is_equal)
-    tt(W("adm"), W("adm0"), W("stand"), OP.mult)
+        ts(W("z4", 5, 6), W("om", 0, 1), -254.0, OP.is_lt)
+    copy(W("xi", 0, 1), idx)
+    ts(W("selt", 0, 512, 4), W("row16"), PM16, OP.is_equal)
+    tt(W("adm"), W("z4", 5, 6), stand, OP.mult)
     ts(W("xi", 1, 2), W("xi", 0, 1), 15, OP.bitwise_and)
     ts(W("xi", 2, 3), W("xi", 0, 1), 5, OP.arith_shift_right)
     for t in range(1, 4):
-        ts(W("selt", t, 512, 4), W("row16"), W("pm16"), OP.is_equal)
+        ts(W("selt", t, 512, 4), W("row16"), PM16, OP.is_equal)
     copy(W("dig", 1, 2), W("xi", 1, 2))
     copy(W("df"), W("xi", 2, 3))
     quant("selq", 0, 128, "selt")
-    ts(W("maskc"), W("basei"), W("ph16"), OP.is_equal, W("adm"), OP.mult)
-    tt(W("dig", 0, 1), W("idx"), W("dig", 1, 2), OP.subtract)
-    ts(W("dig", 2, 3), W("ph16"), -1.0, OP.mult, 128.0, OP.add)
-    ts(W("dig", 3, 4), W("pm16"), -1.0, OP.mult)
+    ts(W("maskc"), W("basei"), PH16, OP.is_equal, W("adm"), OP.mult)
+    tt(W("dig", 0, 1), idx, W("dig", 1, 2), OP.subtract)
+    ts(W("dig", 2, 3), PH16, -1.0, OP.mult, 128.0, OP.add)
+    ts(W("dig", 3, 4), PM16, -1.0, OP.mult)
     fill(W("y2t"), 0.0)
     for t in range(4):
         ts(W("y2t", t, 32, 4), W("maskc"), W("dig", t, t + 1), OP.mult)
@@ -387,13 +406,13 @@ def rank_program(g, core, T, topo):
     mm(4, "selq", 0, "y2q", 0, 128)
     copy(W("base2"), W("base"))
     ts(W("a2"), W("rr", 8, 18, 9), 0.0, OP.is_lt, float(128 + A * r), OP.mult)
-    ts(W("mgv"), W("df"), 96.0, OP.mult, W("idx"), OP.add)
+    ts(W("mgv", 0, 1), W("df"), 96.0, OP.mult, idx, OP.add)
     tt(W("base2", 0, 2), W("base", 0, 2), W("a2"), OP.add)
     tt(W("fl"), W("ps4", 0, 8), W("base2"), OP.add)
-    ts(W("blk"), W("mgv"), 1.0, OP.add, W("adm"), OP.mult)
+    ts(W("mgv", 1, 2), W("mgv", 0, 1), 1.0, OP.add, W("adm"), OP.mult)
     copy(W("fl16"), W("fl"))
-    ts(W("mgc"), W("blk"), -1.0, OP.add)
-    dma("y", "stmg", T.mg[:], T.mgc[:], [W("mgc")], [])
+    ts(W("mgv", 2, 3), W("mgv", 1, 2), -1.0, OP.add)
+    dma("y", "stmg", T.mg[:], ap(W("mgv", 2, 3)), [W("mgv", 2, 3)], [])
     quant("vq", 0, 128, "vt")
 
     pick("gq", 0, "hb", 384, W("fl16"))

from concourse.bass import DstId, RemoteDMATransfer
from concourse.mybir import dt, AluOpType as OP, AxisListType, ActivationFunctionType as AF

N, COLS, A, KM, CAPP = 8, 128, 32, 48, 16
RUN = 20
NONE = RUN * N
BIG = 1e29

SCRATCH = {}


def _bufs():
    def sb(n, w, d="float32"):
        SCRATCH[n] = ("sbuf", [128, w], d)
    for n, w in dict(xa=512, xt=512, wt=2048, vt=512, ebt=2048, trict=512, cht=1024, selt=512, d8t=512, ut=1024, wwt=512,
                     x2t=512, yt=512, it=512, zt=512, mt=512, ht=512, hxt=512, y2t=512, ott=1024,
                     roww=256, io=256, row16=128).items():
        sb(n, w, "bfloat16")
    for n, w in dict(mp=264, neg=256, br=96, tri=96, bb=192, ge=96, gt=96, cs=96, junk=256, idx=2, e9=16, d8=8, d48=8,
                     pm=2, om=3, pay=8, pays=8, y8=8, zer8=8, pc=4, init=1, ord8=8,
                     basei=8, base=8, base2=8, fl=8, a2=2, t96=128, id256=128, rr=36, z4=6, adm=1, df=1,
                     mgv=3, dig=4, yd=32, maskc=8, ysb=128, inf8=8).items():
        sb(n, w)
    for n in ("ci", "xi"):
        sb(n, 3, "int32")
    for n, w in dict(offc=2, off16=16, l2=4, fl16=8).items():
        sb(n, w, "uint16")
    for n, w in dict(qa=128, xw=256, alla=256, wq=512, vq=128, eq=512, tq=128, cq=256, selq=128, d8q=128, uq=256, wwq=128,
                     x2q=128, yq=128, sb=256, lb=288, pk=160, pk2=160, mq=128, hq=128, hb=384, otq=256, y2q=128,
                     gq=128).items():
        sb(n + "c", w, "float8_e4m3fn_x4")
        sb(n + "s", w, "uint8")
    for i in range(8):
        SCRATCH["ps%d" % i] = ("psum", [128, 512], "float32")


_bufs()
DMAS = ["lda", "ldx", "ldw", "ldv", "ownc", "owns", "stmg", "stoc", "st0", "st1", "st2", "st3", "sty"]
SEMAPHORES = ["qv", "qs", "qt", "qg", "arra", "arrb", "arrc", "loca", "locb", "locc"] + DMAS


def rank_program(g, core, T, topo):
    r = T.rank_of(core)
    if r is None:
        return
    eng = {"v": g.vector, "s": g.scalar, "t": g.tensor, "g": g, "y": g.sync}
    count = {"v": 0, "s": 0, "t": 0, "g": 0}
    waited, acc, last = {}, {}, {}

    def W(name, a=0, b=None, step=1, p0=0, p1=128):
        return (name, a, SCRATCH[name][1][1] if b is None else b, step, p0, p1)

    def ap(v):
        name, a, b, step, p0, p1 = v
        return T[name][p0:p1, a:b] if step == 1 else T[name][p0:p1, a:b:step]

    def meet(v, w):
        if v[0][:2] == "ps":
            return True
        if v[4] >= w[5] or w[4] >= v[5] or v[1] >= w[2] or w[1] >= v[2]:
            return False
        return not (v[3] == w[3] and v[3] > 1 and (v[1] - w[1]) % v[3])

    def order(q, reads, writes, sem, val):
        need = {}
        for views, wr in ((reads, False), (writes, True)):
            for v in views:
                for (o, owr, osem, oval, oq) in acc.get(v[0], ()):
                    bank = v[0][:2] == "ps"
                    if oq == q == "t" and bank:
                        continue
                    if not (wr or owr or (bank and oq != q)) or not meet(v, o):
                        continue
                    need[osem] = max(need.get(osem, 0), oval)
        for s in sorted(need):
            wait(q, s, need[s])
        for views, wr in ((reads, False), (writes, True)):
            for v in views:
                acc.setdefault(v[0], []).append((v, wr, sem, val, q))

    def wait(q, sem, val):
        if waited.get((q, sem), 0) < val:
            waited[(q, sem)] = val
            eng[q].wait_ge(T.sem[sem], val)

    def op(q, reads, writes, call):
        count[q] += 1
        sem = "q" + q
        order(q, reads, writes, sem, count[q])
        call().then_inc(T.sem[sem], 1)
        last[sem] = count[q]

    def dma(q, sem, out, in_, reads, writes):
        order(q, reads, writes, sem, 16)
        eng[q].dma_start(out, in_).then_inc(T.sem[sem], 16)
        last[sem] = 16

    def landed(sem, val, views):
        for v in views:
            acc.setdefault(v[0], []).append((v, True, sem, val, "net"))
        last[sem] = val

    def sc(x):
        return ap(x) if isinstance(x, tuple) else x

    def vs(*xs):
        return [x for x in xs if isinstance(x, tuple)]

    def fill(v, c):
        op("v", [], [v], lambda: g.vector.memset(ap(v), c))

    def ts(out, in0, s1, op0, s2=None, op1=None):
        if op1 is None:
            op("v", vs(in0, s1), [out], lambda: g.vector.tensor_scalar(ap(out), ap(in0), sc(s1), None, op0))
        else:
            op("v", vs(in0, s1, s2), [out], lambda: g.vector.tensor_scalar(ap(out), ap(in0), sc(s1), sc(s2), op0, op1))

    def tt(out, a, b, o):
        op("v", [a, b], [out], lambda: g.vector.tensor_tensor(ap(out), ap(a), ap(b), o))

    def copy(out, a):
        op("v", [a], [out], lambda: g.vector.tensor_copy(ap(out), ap(a)))

    def red(out, a, o):
        op("v", [a], [out], lambda: g.vector.tensor_reduce(ap(out), ap(a), AxisListType.X, o))

    def scan(out, d0, d1, init, o0, o1):
        op("v", vs(d0, d1, init), [out], lambda: g.vector.tensor_tensor_scan(ap(out), ap(d0), ap(d1), sc(init), o0, o1))

    def turn(out, a):
        op("v", [a], [out], lambda: g.vector.transpose(ap(out), ap(a)))

    def act(out, a, f, scale=1.0):
        op("s", [a], [out], lambda: g.scalar.activation(ap(out), ap(a), f, scale=scale))

    def acol(out, a, col):
        op("s", [a, col], [out], lambda: g.scalar.activation(ap(out), ap(a), AF.Identity, scale=ap(col)))

    def asum(out, a, total):
        op("s", [a], [out, total], lambda: g.scalar.activation(ap(out), ap(a), AF.Relu, scale=-1.0, accum_out=ap(total)))

    def zero(n):
        for k in range(0, SCRATCH[n][1][1], 512):
            act(W(n, k, k + 512), W("zt"), AF.Copy)

    def quant(q, a, b, tile, c=0):
        n = b - a
        oc, os_, t = W(q + "c", a, b), W(q + "s", a, b), W(tile, c, c + 4 * n)
        op("v", [t], [oc, os_], lambda: g.vector.quantize_mx(ap(oc), ap(os_), ap(t)))

    def mm(bank, st, a, mv, b, n, start=True, stop=True):
        o = W("ps%d" % bank, 0, n)
        l, ls, m, ms = W(st + "c", a, a + 128), W(st + "s", a, a + 128), W(mv + "c", b, b + n), W(mv + "s", b, b + n)
        op("t", [l, ls, m, ms], [o], lambda: g.tensor.matmul_mx(ap(o), ap(l), ap(ls), ap(m), ap(ms), start, stop))

    def pick(dst, a, src, w, off):
        n = 16 * (off[2] - off[1])
        oc, os_, ic, is_ = W(dst + "c", a, a + n), W(dst + "s", a, a + n), W(src + "c", 0, w), W(src + "s", 0, w)
        op("v", [ic, off], [oc], lambda: g.vector.tensor_copy(ap(oc).bitcast(dt.uint32), ap(ic).bitcast(dt.uint32).indirect(ap(off))))
        op("s", [is_, off], [os_], lambda: g.scalar.activation(ap(os_), ap(is_).indirect(ap(off)), AF.Copy))

    def iota(out, pattern, base, cm):
        if SCRATCH[out[0]][2] == "int32":
            op("g", [], [out], lambda: g.iota(ap(out), pattern, base, cm))
        else:
            op("g", [], [out], lambda: g.iota(ap(out), pattern, base, cm, allow_small_or_imprecise_dtypes=True))

    others = [(r + k) % N for k in range(1, N)]
    away = [e for e in range(16) if all(e in topo.engines(core, T.cores[d]) for d in others)]

    def bits(es):
        return sum(1 << e for e in es)

    def dst_id(d):
        rid, pid = topo.addr(T.cores[d], core)
        return DstId(rid=rid, pnc=pid)

    def send(x, parts, arr, loc):
        tr = []
        for ds, s, o, es in parts:
            order("g", [s], [], loc, 0)
            sv, ov = ap(s), ap(o)
            if x == "c":
                sv, ov = sv.bitcast(dt.uint8), ov.bitcast(dt.uint8)
            tr.append(RemoteDMATransfer(dst_ids=[dst_id(d) for d in ds], dma_engine_mask=bits(es), remote_sem=T.sem[arr],
                                        srcs=[sv], dsts=[ov for d in ds]))
        g.remote_dma_fused(tr, local_sem=T.sem[loc])
        last[loc] = last.get(loc, 0) + sum(len(p[3]) for p in parts)

    def everyone(src, a, dst, b, n, arr, loc):
        for x in "cs":
            send(x, [(others, W(src + x, a, a + n), W(dst + x, b, b + n), away)], arr, loc)
        return 2 * len(away) * (N - 1)

    dma("y", "lda", T.xa[:, 0:4 * A], T.x[:, 0:4 * A], [], [W("xa", 0, 4 * A)])
    dma("y", "ldx", T.xt[:], T.x[:], [], [W("xt")])
    PCOL, PM16, P32, PH16 = [W("pc", i, i + 1) for i in range(4)]
    iota(W("ci", 0, 1), [[0, 1]], 0, 1)
    iota(PCOL, [[0, 1]], 0, 1)
    iota(W("basei"), [[16, 8]], 0, 0)
    iota(W("io"), [[1, 256]], 0, 0)
    iota(W("row16"), [[0, 8], [1, 16]], 0, 0)
    fill(W("zt"), 0.0)
    fill(W("xa", 4 * A, 512), 0.0)
    for n in ("wwt", "x2t", "yt", "it"):
        zero(n)
    ts(W("ci", 1, 2), W("ci", 0, 1), 15, OP.bitwise_and)
    ts(W("ci", 2, 3), W("ci", 0, 1), 31, OP.bitwise_and)
    copy(PM16, W("ci", 1, 2))
    copy(P32, W("ci", 2, 3))
    ts(W("base"), W("basei"), PM16, OP.add)
    tt(PH16, PCOL, PM16, OP.subtract)
    copy(W("offc"), W("base", 0, 2))
    fill(W("neg"), -BIG)
    fill(W("mp", 0, 1), -BIG)
    fill(W("bb"), -BIG)
    quant("qa", 0, 128, "xa")
    n_a = everyone("qa", 0, "alla", A * r, A, "arra", "loca")
    landed("arra", n_a, [W("alla" + x, A * d, A * d + A) for d in others for x in "cs"])
    wait("y", "loca", last["loca"])
    dma("y", "ldw", T.wt[:], T.w[:], [], [W("wt")])
    dma("y", "ldv", T.vt[:], T.v[:], [], [W("vt")])
    iota(W("roww"), [[0, 8], [1, 16], [0, 2]], -256, 0)
    iota(W("ord8"), [[-1, 2], [0, 4]], 256, 0)
    pick("alla", A * r, "qa", 128, W("offc"))
    quant("xw", 0, 128, "xt")
    fill(W("d8t"), 0.0)
    fill(W("ut"), 0.0)
    for n in ("ebt", "ott"):
        zero(n)
    fill(W("tri", 0, 32), BIG)
    ts(W("tri", 32, 64), W("io", 0, 32), P32, OP.is_gt, 2 * BIG, OP.mult)
    ts(W("tri", 64, 96), W("io", 0, 32), P32, OP.is_lt, 2 * BIG, OP.mult)
    ts(W("tri", 32, 96), W("tri", 32, 96), -BIG, OP.add)
    fill(W("trict"), 0.0)
    ts(W("t96"), W("io", 0, 128), PCOL, OP.is_gt)
    ts(W("id256"), W("io", 0, 128), PCOL, OP.is_equal, -256.0, OP.mult)
    tt(W("trict", 0, 512, 4), W("t96"), W("id256"), OP.add)
    quant("tq", 0, 128, "trict")
    fill(W("init"), 0.0)
    fill(W("init", 0, 1, 1, 0, A), 1000.0)
    fill(W("zer8"), 0.0)
    ts(W("inf8"), W("zer8"), PM16, OP.add, 3.0, OP.min)
    ts(W("off16", 1, 16, 2), W("inf8"), 128.0, OP.add)
    m = N - r
    fill(W("pay"), 1.0)
    fill(W("pay", 0, 8, 4), -16.0 * m)
    fill(W("pay", 1, 8, 4), -4.0 * m)
    for i in range(4):
        ts(W("ebt", 512 * i + i, 512 * i + 512, 4), W("io", 0, 128), PCOL, OP.is_equal)
    quant("eq", 0, 512, "ebt")

    mm(0, "xw", 0, "alla", 0, 256)
    b = W("mp", 256, 257)
    scan(W("mp", 1, 257), W("ps0", 0, 256), W("neg"), -BIG, OP.max, OP.max)
    idx, offr, pm, stand = W("idx", 0, 1), W("idx", 1, 2), W("pm", 0, 1), W("pm", 1, 2)
    op("s", [W("mp", 1, 257), b], [W("junk"), idx],
       lambda: g.scalar.activation(T.junk[:], T.mp[:, 1:257], AF.Sign, bias=ap(b), scale=-1.0, accum_out=ap(idx)))
    ts(W("br"), W("tri"), b, OP.min)
    ts(W("e9", 0, 9), W("mp", 0, 257, 32), b, OP.is_lt)
    turn(W("bb", 64, 128), W("br", 32, 96))
    for me, him, at in ((1, 2, 128), (1, 3, 160), (2, 1, 32), (2, 3, 128), (3, 1, 32), (3, 2, 0)):
        turn(W("bb", at, at + 32, 1, 32 * me, 32 * me + 32), W("br", 0, 32, 1, 32 * him, 32 * him + 32))
    tt(W("d8"), W("e9", 0, 8), W("e9", 1, 9), OP.subtract)
    act(W("d48"), W("d8"), AF.Copy, float(KM))
    acol(W("x2t", 0, 32, 4), W("d8"), PH16)
    acol(W("x2t", 2, 32, 4), W("d8"), PM16)
    ts(W("ge"), W("bb", 0, 96), b, OP.is_ge)
    ts(W("gt"), W("bb", 96, 192), b, OP.is_gt)
    scan(W("cs"), W("ge"), W("gt"), W("init"), OP.add, OP.add)
    c = W("cs", 95, 96)
    ts(W("d8t", 0, 32, 4), W("d48"), c, OP.is_gt)
    ts(offr, c, float(KM), OP.is_lt)
    quant("d8q", 0, 128, "d8t")
    mm(1, "tq", 0, "d8q", 0, 128)
    for h in range(2):
        ts(W("ut", 512 * h, 512 * h + 512, 4), W("io", 128 * h, 128 * h + 128), idx, OP.is_equal, offr, OP.mult)
        quant("uq", 128 * h, 128 * h + 128, "ut", 512 * h)
        mm(2 + 2 * h, "tq", 0, "uq", 128 * h, 128)
    red(pm, W("ps1", 0, 8), OP.min)
    ts(W("wwt", 0, 512, 2), W("roww"), pm, OP.is_equal)
    ts(stand, pm, -256.0 + CAPP, OP.is_lt)
    ts(W("pay", 2, 8, 4), W("zer8", 0, 2), pm, OP.add, 256.0, OP.add)
    quant("wwq", 0, 128, "wwt")
    quant("x2q", 0, 128, "x2t")
    mm(3, "wwq", 0, "x2q", 0, 128)
    ts(W("pays"), W("pay"), stand, OP.mult)
    for h in range(2):
        asum(W("junk", 0, 128), W("ps%d" % (2 + 2 * h), 0, 128), W("om", 1 + h, 2 + h))
    ts(W("y8"), W("ord8"), W("om", 1, 2), OP.subtract, W("om", 2, 3), OP.is_equal)
    tt(W("yt", 0, 32, 4), W("y8"), W("pays"), OP.mult)
    quant("yq", 0, 128, "yt")
    mm(0, "uq", 0, "yq", 0, 128)
    mm(1, "uq", 128, "yq", 0, 128)
    copy(W("off16", 0, 16, 2), W("ps3", 0, 8))
    copy(W("it", 0, 8), W("ps0", 0, 8))
    act(W("it", 8, 16), W("ps1", 0, 8), AF.Copy)
    quant("xw", 128, 256, "it")
    pick("sb", 0, "xw", 256, W("off16"))
    e = away
    groups = {"c": ((0, e[0:2]), (1, e[2:4]), (2, e[4:6]), (3, e[6:8]), (4, e[0:2]), (5, e[2:4]), (6, e[4:8])),
              "s": ((0, e[0:2]), (1, e[2:4]), (2, e[4:6]), (3, e[6:8]), (4, e[4:6]), (5, e[6:8]), (6, e[0:4]))}
    for x in "cs":
        for part in (groups[x][:4], groups[x][4:]):
            send(x, [([others[k]], W("sb" + x, 32 * others[k], 32 * others[k] + RUN), W("lb" + x, RUN * r, RUN * r + RUN), es)
                     for k, es in part], "arrb", "locb")
    n_b = sum(len(es) for x in "cs" for k, es in groups[x])
    landed("arrb", n_b, [W("lb" + x, RUN * d, RUN * d + RUN) for d in others for x in "cs"])
    sc_, ss_ = W("sbc", 32 * r, 32 * r + RUN), W("sbs", 32 * r, 32 * r + RUN)
    lc_, ls_ = W("lbc", RUN * r, RUN * r + RUN), W("lbs", RUN * r, RUN * r + RUN)
    dma("y", "ownc", ap(lc_).bitcast(dt.uint8), ap(sc_).bitcast(dt.uint8), [sc_], [lc_])
    dma("s", "owns", ap(ls_), ap(ss_), [ss_], [ls_])
    for h in range(2):
        mm(2 + h, "uq", 128 * h, "eq", 0, 128)
    for h in range(2):
        act(W("ott", 512 * h + 3, 512 * h + 512, 4), W("ps%d" % (2 + h), 0, 128), AF.Copy)
    quant("wq", 0, 512, "wt")
    for i in range(4):
        mm(4 + i, "wq", 128 * i, "xw", 0, 128)
    for i in range(4):
        act(W("hxt", i, 512, 4), W("ps%d" % (4 + i), 0, 128), AF.Relu, 0.0625)
    quant("otq", 0, 256, "ott")
    ts(W("om", 0, 1), W("om", 1, 2), -1.0, OP.mult, W("om", 2, 3), OP.subtract)
    quant("hb", 0, 128, "hxt")
    for i in range(4):
        mm(4 + i, "eq", 128 * i, "xw", 0, 128, True, False)
    for n in ("cht", "mt", "ht"):
        zero(n)
    fill(W("rr"), 0.0)
    quant("lb", NONE, NONE + 128, "zt")
    quant("pk", 32, 160, "zt")
    quant("pk2", 32, 160, "zt")
    for h in range(2):
        for t in range(3):
            ts(W("cht", 512 * h + t, 512 * h + 512, 4), W("row16"), float((A * r) % 128 + 16 * h), OP.add, PCOL, OP.is_equal)
    quant("cq", 0, 256, "cht")

    for h in range(2):
        mm(h, "cq", 128 * h, "lb", 0, RUN * N)
    for h in range(2):
        mm(2 + h, "otq", 128 * h, "lb", 0, RUN * N)
    o1 = CAPP + 2 * (r // 4)

    def ent(h, o):
        return W("ps%d" % h, o1 + o, RUN * N, RUN)
    for h in range(2):
        scan(W("rr", 9 * h + 1, 9 * h + 9), ent(h, 0), W("zer8"), 0.0, OP.min, OP.min)
    ts(W("l2", 0, 2), W("rr", 8, 18, 9), float(NONE), OP.add)
    pick("pk", 0, "lb", 288, W("l2", 0, 2))
    for h in range(2):
        tt(W("rr", 19 + 9 * h, 27 + 9 * h), ent(h, 0), W("rr", 9 * h, 9 * h + 8), OP.max)
    for h in range(2):
        scan(W("yd", 8 * h, 8 * h + 8), W("rr", 19 + 9 * h, 27 + 9 * h), ent(h, 1), 0.0, OP.min, OP.min)
    ts(W("l2", 2, 4), W("yd", 7, 16, 8), float(NONE), OP.add)
    pick("pk2", 0, "lb", 288, W("l2", 2, 4))
    for i in range(4):
        mm(4 + i, "eq", 128 * i, "pk", 0, 128, False, False)
    for i in range(4):
        mm(4 + i, "eq", 128 * i, "pk2", 0, 128, False, True)
    if r:
        for h in range(2):
            for o in range(2):
                red(W("z4", 2 * h + o, 2 * h + o + 1), W("ps%d" % (2 + h), CAPP + 2 * h + o, RUN * r, RUN), OP.add)
    for i in range(4):
        o, p = W("mt", i, 128, 4), W("ps%d" % (4 + i), 0, 32)
        if i % 2:
            ts(o, p, 0.5, OP.mult)
        else:
            act(o, p, AF.Copy, 0.5)
    quant("mq", 0, 128, "mt")
    for i in range(4):
        mm(i, "wq", 128 * i, "mq", 0, 128)
    for i in range(4):
        o, p = W("ht", i, 128, 4), W("ps%d" % i, 0, 32)
        if i % 2:
            ts(o, p, 0.0, OP.max, 0.0625, OP.mult)
        else:
            act(o, p, AF.Relu, 0.0625)
    quant("hq", 0, 128, "ht")
    n_c = everyone("hq", 0, "hb", 128 + A * r, A, "arrc", "locc")
    landed("arrc", n_c, [W("hb" + x, 128 + A * d, 128 + A * d + A) for d in others for x in "cs"])
    pick("hb", 128 + A * r, "hq", 128, W("offc"))
    if r:
        red(W("z4", 4, 5), W("z4", 0, 4), OP.add)
        ts(W("z4", 5, 6), W("z4", 4, 5), W("om", 0, 1), OP.add, -254.0, OP.is_lt)
    else:
        ts(W("z4", 5, 6), W("om", 0, 1), -254.0, OP.is_lt)
    copy(W("xi", 0, 1), idx)
    ts(W("selt", 0, 512, 4), W("row16"), PM16, OP.is_equal)
    tt(W("adm"), W("z4", 5, 6), stand, OP.mult)
    ts(W("xi", 1, 2), W("xi", 0, 1), 15, OP.bitwise_and)
    ts(W("xi", 2, 3), W("xi", 0, 1), 5, OP.arith_shift_right)
    for t in range(1, 4):
        ts(W("selt", t, 512, 4), W("row16"), PM16, OP.is_equal)
    copy(W("dig", 1, 2), W("xi", 1, 2))
    copy(W("df"), W("xi", 2, 3))
    quant("selq", 0, 128, "selt")
    ts(W("maskc"), W("basei"), PH16, OP.is_equal, W("adm"), OP.mult)
    tt(W("dig", 0, 1), idx, W("dig", 1, 2), OP.subtract)
    ts(W("dig", 2, 3), PH16, -1.0, OP.mult, 128.0, OP.add)
    ts(W("dig", 3, 4), PM16, -1.0, OP.mult)
    fill(W("y2t"), 0.0)
    for t in range(4):
        ts(W("y2t", t, 32, 4), W("maskc"), W("dig", t, t + 1), OP.mult)
    quant("y2q", 0, 128, "y2t")
    mm(4, "selq", 0, "y2q", 0, 128)
    copy(W("base2"), W("base"))
    ts(W("a2"), W("rr", 8, 18, 9), 0.0, OP.is_lt, float(128 + A * r), OP.mult)
    ts(W("mgv", 0, 1), W("df"), 96.0, OP.mult, idx, OP.add)
    tt(W("base2", 0, 2), W("base", 0, 2), W("a2"), OP.add)
    tt(W("fl"), W("ps4", 0, 8), W("base2"), OP.add)
    ts(W("mgv", 1, 2), W("mgv", 0, 1), 1.0, OP.add, W("adm"), OP.mult)
    copy(W("fl16"), W("fl"))
    ts(W("mgv", 2, 3), W("mgv", 1, 2), -1.0, OP.add)
    dma("y", "stmg", T.mg[:], ap(W("mgv", 2, 3)), [W("mgv", 2, 3)], [])
    quant("vq", 0, 128, "vt")

    pick("gq", 0, "hb", 384, W("fl16"))
    dma("y", "stoc", T.oc[:], T.gqc[:].bitcast(dt.uint8), [W("gqc")], [])
    for k in range(4):
        v = W("gqs", 0, 128, 1, 32 * k, 32 * k + 4)
        dma("s", "st%d" % k, T.osc[4 * k:4 * k + 4, :], ap(v), [v], [])
    mm(5, "vq", 0, "gq", 0, 128)
    copy(W("ysb"), W("ps5", 0, 128))
    dma("y", "sty", T.y[:], T.ysb[:], [W("ysb")], [])
    for s in sorted(last):
        wait("g", s, last[s])
